import numpy as np
import ml_dtypes


def mxq(x, axis, fmt="e4m3"):
    dtype, down = {"e4m3": (ml_dtypes.float8_e4m3fn, 7), "e5m2": (ml_dtypes.float8_e5m2, 14)}[fmt]
    v = np.moveaxis(np.asarray(x, np.float32).astype(ml_dtypes.bfloat16).astype(np.float64), axis, -1)
    blocks = v.reshape(v.shape[:-1] + (-1, 32))
    amax = np.abs(blocks).max(-1, keepdims=True)
    byte = np.maximum(np.where(amax > 0, np.frexp(amax)[1] - 1 + 127, 0) - down, 1)
    scale = np.exp2(byte - 127.0)
    codes = (blocks / scale).astype(np.float32).astype(dtype).astype(np.float64)
    return np.moveaxis((codes * scale).reshape(v.shape), -1, axis)


WIDE = False


def mx_kscale(k):
    if not WIDE:
        return np.ones(k)
    levels = np.array([30, -30])
    if k % 512:
        return np.exp2(np.random.permutation(np.resize(levels, k // 32))).repeat(32)
    a = np.empty((k // 512, 16))
    for p in range(k // 512):
        a[p, :8] = np.random.permutation(np.resize(levels, 8))
        for g in range(8):
            far = levels[np.abs(levels - a[p, g]) >= 10]
            a[p, g + 8] = far[np.random.randint(len(far))]
    return np.exp2(a.ravel()).repeat(32)


def f64(x):
    return np.asarray(x).astype(np.float64)


def striped(idx):
    return np.tile(np.asarray(idx).reshape(-1, 16).T, (8, 1)).astype(np.uint16)


def unstriped(offs):
    return offs[:16].T.reshape(-1).astype(np.int64)


E2M1 = np.array([0.0, 0.5, 1.0, 1.5, 2.0, 3.0, 4.0, 6.0, -0.0, -0.5, -1.0, -1.5, -2.0, -3.0, -4.0, -6.0])


def pack_weight(w, fmt):
    k, n = w.shape
    w = f64(np.asarray(w, np.float32).astype(ml_dtypes.bfloat16)).reshape(k // 32, 32, n)
    amax = np.abs(w).max(1)
    if fmt in ("e4m3", "e5m2"):
        byte = np.frexp(amax)[1] - 1 + 127 - (7 if fmt == "e4m3" else 14)
    else:
        mant, ex = np.frexp(amax / 6.0)
        byte = np.where(mant > 0.5, ex, ex - 1) + 127
    byte = np.clip(np.where(amax > 0, byte, 1), 1, 254)
    scaled = (w * np.exp2(127.0 - byte)[:, None, :]).reshape(k, n).astype(np.float32)
    by_word = np.ascontiguousarray(scaled.reshape(k // 512, 128, 4, n).transpose(0, 1, 3, 2))
    if fmt in ("e4m3", "e5m2"):
        words = by_word.astype(ml_dtypes.float8_e4m3fn if fmt == "e4m3" else ml_dtypes.float8_e5m2).view(np.uint8)
    else:
        c = by_word.astype(ml_dtypes.float4_e2m1fn).view(np.uint8) & 0xF
        words = (c[..., 0::2] | (c[..., 1::2] << 4)).reshape(k // 512, 128, 2 * n)
    return np.ascontiguousarray(words), np.ascontiguousarray(byte.astype(np.uint8).reshape(k // 512, 16, n))


def unpack_weight(words, scales, fmt):
    g, _, n = scales.shape
    words = np.ascontiguousarray(words).reshape(g, 128, n, -1)
    if fmt in ("e4m3", "e5m2"):
        vals = words.view(ml_dtypes.float8_e4m3fn if fmt == "e4m3" else ml_dtypes.float8_e5m2).astype(np.float64)
    else:
        nib = np.empty((g, 128, n, 4), np.uint8)
        nib[..., 0::2] = words & 0xF
        nib[..., 1::2] = words >> 4
        vals = E2M1[nib]
    vals = vals * np.repeat(np.exp2(scales.astype(np.float64) - 127.0), 8, axis=1)[..., None]
    return vals.transpose(0, 1, 3, 2).reshape(g * 512, n)


K, T, J, R, F, Z, C, D, O, N = 512, 1024, 256, 512, 512, 1024, 512, 512, 256, 256


def setup_inputs():
    n = np.random.standard_normal
    idx = np.random.permutation(T)[:J]
    idx2 = np.random.permutation(Z)[:J]
    idx3 = np.random.permutation(C)[:J]
    idx4 = np.random.permutation(D)[:J]
    idx5 = np.random.permutation(C)[:O]
    idx6 = np.random.permutation(D)[:O]
    idx7 = np.random.permutation(T)[:O]
    fk = mx_kscale(K)
    ff = mx_kscale(F)
    fr = mx_kscale(R)
    xtp = pack_weight(n((K, T)) / fk[:, None], "e2m1")
    xop = pack_weight(n((F, Z)) / ff[:, None], "e5m2")
    wp = pack_weight(n((K, R)) * 1 / np.sqrt(K) * fk[:, None] * fr, "e5m2")
    w0p = pack_weight(n((F, R)) * 1 / np.sqrt(F) * ff[:, None] * fr, "e4m3")
    w2p = pack_weight(n((F, R)) * 1 / np.sqrt(F) * ff[:, None], "e4m3")
    wbp = pack_weight(n((R, N)) * 1 / np.sqrt(R) / fr[:, None], "e4m3")
    wsp = pack_weight(n((K, N)) * 1 / np.sqrt(K) * fk[:, None], "e4m3")
    return {
        "xt_words": xtp[0],
        "xt_scales": xtp[1],
        "xo_words": xop[0],
        "xo_scales": xop[1],
        "w_words": wp[0],
        "w_scales": wp[1],
        "w0_words": w0p[0],
        "w0_scales": w0p[1],
        "w2_words": w2p[0],
        "w2_scales": w2p[1],
        "wb_words": wbp[0],
        "wb_scales": wbp[1],
        "ws_words": wsp[0],
        "ws_scales": wsp[1],
        "offs": striped(idx),
        "offs2": striped(idx2),
        "offs3": striped(idx3),
        "offs4": striped(idx4),
        "offs5": striped(idx5),
        "offs6": striped(idx6),
        "offs7": striped(idx7),
    }


def reference(xt_words, xt_scales, xo_words, xo_scales, w_words, w_scales, w0_words, w0_scales, w2_words, w2_scales, wb_words, wb_scales, ws_words, ws_scales, offs, offs2, offs3, offs4, offs5, offs6, offs7):
    idx = unstriped(offs)
    idx2 = unstriped(offs2)
    idx3 = unstriped(offs3)
    idx4 = unstriped(offs4)
    idx5 = unstriped(offs5)
    idx6 = unstriped(offs6)
    idx7 = unstriped(offs7)
    xtu = unpack_weight(xt_words, xt_scales, "e2m1")
    xou = unpack_weight(xo_words, xo_scales, "e5m2")
    wu = unpack_weight(w_words, w_scales, "e5m2")
    w0u = unpack_weight(w0_words, w0_scales, "e4m3")
    w2u = unpack_weight(w2_words, w2_scales, "e4m3")
    wbu = unpack_weight(wb_words, wb_scales, "e4m3")
    wsu = unpack_weight(ws_words, ws_scales, "e4m3")
    xtidxg = xtu[:, idx]
    xoidx2g = xou[:, idx2]
    a = wu.T @ xtidxg + w0u.T @ xoidx2g
    b = w2u.T @ xoidx2g
    lb = b[:, 0:1]
    la = a[:, 0:1]
    pw = np.zeros((R, C))
    pw[:, idx3] = a
    pv = np.zeros((R, D))
    pv[:, idx4] = b
    hid = np.maximum(pw[:, idx5] * lb, pv[:, idx6] * la)
    hidq = mxq(hid, 0, "e5m2")
    xtidx7g = xtu[:, idx7]
    y = wbu.T @ hidq + wsu.T @ xtidx7g
    return y

from contextlib import ExitStack

import concourse.mybir as mybir

K, T, J, R, F, Z, C, D, O, N = 512, 1024, 256, 512, 512, 1024, 512, 512, 256, 256
FLOPS = 2 * (K * R * J + 2 * F * R * J + R * N * O + K * N * O)

F32, BF16 = mybir.dt.float32, mybir.dt.bfloat16
I32, U32, U16, U8 = mybir.dt.int32, mybir.dt.uint32, mybir.dt.uint16, mybir.dt.uint8
E4M3, E5M2, E2M1 = mybir.dt.float8_e4m3fn_x4, mybir.dt.float8_e5m2_x4, mybir.dt.float4_e2m1fn_x4
COPY = mybir.ActivationFunctionType.Copy
MAX = mybir.AluOpType.max

P = 128
PACK = 4
QUAD = 32
HALF = O // 2
SPLIT = 128


def tile_list_leadboards_noted_further_plain_kernel(
    tc, xt_words, xt_scales, xo_words, xo_scales, w_words, w_scales, w0_words, w0_scales, w2_words, w2_scales,
    wb_words, wb_scales, ws_words, ws_scales, offs, offs2, offs3, offs4, offs5, offs6, offs7, out,
):
    nc = tc.nc
    with ExitStack() as ctx:
        pool = ctx.enter_context(tc.tile_pool(name="sbuf", bufs=1))
        psum = ctx.enter_context(tc.psum_pool(name="psum", bufs=1))

        def sb(name, shape, dtype, reuse=None):
            return pool.tile(shape, dtype, name=name, tag=reuse or name, align_bytes=64)

        def load_list(name, src):
            tile = pool.tile([P, 16], U16, name=name)
            nc.sync.dma_start(tile[:], src)
            return tile

        def load_words(name, src, cols):
            tile = sb(name, [P, cols], U32)
            nc.sync.dma_start(tile[:].bitcast(I32), src[0].rearrange("p n t -> p (n t)").bitcast(I32))
            return tile

        def zero_plane(name, cols):
            plane = sb(name, [P, cols], U8)
            nc.gpsimd.memset(plane[:].bitcast(I32), 0)
            return plane

        def stage_scales(queue, name, src, cols):
            stage = sb(name, [4, 4, cols // 4], I32)
            queue.dma_start(stage[:], src[0].bitcast(I32).rearrange("(q r) c -> r q c", r=4))
            return stage

        def spread(plane, stage):
            for q in range(4):
                nc.vector.tensor_copy(plane[QUAD * q : QUAD * q + 4, :].bitcast(I32), stage[:, q, :])

        def load_plane(queue, plane, src):
            for q in range(4):
                queue.dma_start(plane[QUAD * q : QUAD * q + 4, :].bitcast(I32), src[0, 4 * q : 4 * q + 4, :].bitcast(I32))

        def deal_words(name, words):
            dealt = sb(name, [P, R], U32)
            nc.scalar.copy(dealt[:].rearrange("p (t m) -> p m t", t=PACK), words[:].rearrange("p (m t) -> p m t", t=PACK))
            return dealt

        def deal_plane(name, plane):
            dealt = sb(name, [P, R], U8)
            nc.vector.tensor_copy(dealt[:].rearrange("p (t m) -> p t m", t=PACK), plane[:].rearrange("p (m t) -> p t m", t=PACK))
            return dealt

        def gather(name, window, offsets, dtype, reuse=None):
            picked = sb(name, [P, J], dtype, reuse)
            nc.vector.tensor_copy(picked[:], window[:].indirect(offsets[:]))
            return picked

        xo_plane = zero_plane("xo_plane", Z)
        w2_plane = zero_plane("w2_plane", R)
        xt_plane = zero_plane("xt_plane", T)
        w0_plane = zero_plane("w0_plane", R)
        w_plane = zero_plane("w_plane", R)
        wb_plane = zero_plane("wb_plane", N)
        ws_plane = zero_plane("ws_plane", N)
        w2_stage = stage_scales(nc.sync, "w2_stage", w2_scales, R)
        l2 = load_list("l2", offs2)
        xo_w = load_words("xo_w", xo_words, Z)
        w2_w = load_words("w2_w", w2_words, R)
        load_plane(nc.scalar, xo_plane, xo_scales)
        w0_w = load_words("w0_w", w0_words, R)
        w_w = load_words("w_w", w_words, R)
        xt_w = sb("xt_w", [P, T], U16)
        nc.sync.dma_start(xt_w[:].bitcast(I32), xt_words[0].bitcast(I32))
        l4 = load_list("l4", offs4)
        l1 = load_list("l1", offs)
        load_plane(nc.sync, xt_plane, xt_scales)
        load_plane(nc.sync, w0_plane, w0_scales)
        load_plane(nc.sync, w_plane, w_scales)
        l3 = load_list("l3", offs3)
        l6 = load_list("l6", offs6)
        l5 = load_list("l5", offs5)
        l7 = load_list("l7", offs7)
        ws_w = load_words("ws_w", ws_words, N)
        wb_w = load_words("wb_w", wb_words, N)
        load_plane(nc.sync, ws_plane, ws_scales)
        load_plane(nc.sync, wb_plane, wb_scales)
        pv = [sb("pv%d" % t, [P, D], F32) for t in range(2)]
        for board in pv:
            nc.vector.memset(board[:], 0.0)

        spread(w2_plane, w2_stage)
        w2_ds = deal_plane("w2_ds", w2_plane)
        xo_gs = gather("xo_gs", xo_plane, l2, U8)
        xo_gw = gather("xo_gw", xo_w, l2, U32)
        w2_dw = deal_words("w2_dw", w2_w)
        w0_dw = deal_words("w0_dw", w0_w)
        w_dw = deal_words("w_dw", w_w)
        pw = [pool.tile([P, C], F32, name="pw%d" % t, tag=old, align_bytes=64) for t, old in enumerate(("w2_w", "xo_w", "w0_w", "w_w"))]
        for board in pw:
            nc.gpsimd.memset(board[:], 0.0)
        b_ps = [psum.tile([P, J], F32, name="b_ps%d" % t, tag="bank%d" % t) for t in range(PACK)]
        for t in range(PACK):
            cols = slice(t * P, (t + 1) * P)
            nc.tensor.matmul_mx(b_ps[t][:], w2_dw[:, cols].bitcast(E4M3), w2_ds[:, cols], xo_gw[:].bitcast(E5M2), xo_gs[:], start=True, stop=True)
        b_sb = [sb("b_sb%d" % t, [P, J], F32) for t in range(PACK)]
        for t in range(PACK):
            nc.scalar.copy(b_sb[t][:], b_ps[t][:])

        def put_scalar(board, offsets, values, lo=0, hi=J):
            nc.scalar.activation(board[:].indirect(offsets[:, lo // 16 : hi // 16]), values[:, lo:hi], COPY)

        def put_vector(board, offsets, values, lo=0, hi=J):
            nc.vector.tensor_copy(board[:].indirect(offsets[:, lo // 16 : hi // 16]), values[:, lo:hi])

        xt_gs = gather("xt_gs", xt_plane, l1, U8)
        put_vector(pv[1], l4, b_sb[1])
        put_scalar(pv[0], l4, b_sb[0])
        w0_ds = deal_plane("w0_ds", w0_plane)
        w_ds = deal_plane("w_ds", w_plane)
        xt_gw = gather("xt_gw", xt_w, l1, U16)
        a_ps = [psum.tile([P, J], F32, name="a_ps%d" % t) for t in range(PACK)]
        for t in range(PACK):
            cols = slice(t * P, (t + 1) * P)
            nc.tensor.matmul_mx(a_ps[t][:], w0_dw[:, cols].bitcast(E4M3), w0_ds[:, cols], xo_gw[:].bitcast(E5M2), xo_gs[:], start=True, stop=False)
        for t in range(PACK):
            cols = slice(t * P, (t + 1) * P)
            nc.tensor.matmul_mx(a_ps[t][:], w_dw[:, cols].bitcast(E5M2), w_ds[:, cols], xt_gw[:].bitcast(E2M1), xt_gs[:], start=False, stop=True)
        pv = pv + [sb("pv2", [P, D], F32, "w_dw"), sb("pv3", [P, D], F32, "w_plane")]
        nc.gpsimd.memset(pv[3][:], 0.0)
        nc.gpsimd.memset(pv[2][:], 0.0)
        a_sb = [sb("a_sb%d" % t, [P, J], F32) for t in range(PACK)]

        g1 = sb("g1", [P, PACK, O], F32)
        g2 = sb("g2", [P, PACK, O], F32)

        def fetch(dst, board, offsets, lead, t, lo, hi):
            nc.scalar.activation(dst[:, t, lo:hi], board[t][:].indirect(offsets[:, lo // 16 : hi // 16]), COPY, scale=lead[t][:, 0:1])

        put_vector(pv[3], l4, b_sb[3])
        for t in range(PACK):
            nc.scalar.copy(a_sb[t][:], a_ps[t][:])
        put_scalar(pv[2], l4, b_sb[2])
        for t in range(3):
            put_vector(pw[t], l3, a_sb[t])
        put_vector(pw[3], l3, a_sb[3], 0, SPLIT)
        for t in (0, 1, 3, 2):
            fetch(g2, pv, l6, a_sb, t, 0, O)
        for t in range(3):
            fetch(g1, pw, l5, b_sb, t, 0, O)
        put_scalar(pw[3], l3, a_sb[3], SPLIT, J)
        fetch(g1, pw, l5, b_sb, 3, 0, HALF)
        fetch(g1, pw, l5, b_sb, 3, HALF, O)

        x7_gs = gather("x7_gs", xt_plane, l7, U8, "a_sb1")
        x7_gw = gather("x7_gw", xt_w, l7, U16, "a_sb2")
        y_ps = [psum.tile([P, 2, HALF], F32, name="y_ps%d" % h, tag="bank%d" % h) for h in range(2)]
        for h in range(2):
            reads = slice(h * HALF, (h + 1) * HALF)
            for u in range(2):
                cols = slice(u * P, (u + 1) * P)
                nc.tensor.matmul_mx(y_ps[h][:, u, :], ws_w[:, cols].bitcast(E4M3), ws_plane[:, cols], x7_gw[:, reads].bitcast(E2M1), x7_gs[:, reads], start=(u == 0), stop=False)
        hid = [sb("hid%d" % h, [P, HALF * PACK], BF16) for h in range(2)]
        hid_w = [sb("hid_w%d" % h, [P, HALF], U32) for h in range(2)]
        hid_s = [sb("hid_s%d" % h, [P, HALF], U8) for h in range(2)]
        for h in range(2):
            reads = slice(h * HALF, (h + 1) * HALF)
            nc.vector.tensor_tensor(
                hid[h][:].rearrange("p (c i t) -> p c t i", i=4, t=PACK),
                g1[:, :, reads].rearrange("p t (c i) -> p c t i", i=4),
                g2[:, :, reads].rearrange("p t (c i) -> p c t i", i=4),
                MAX,
            )
        for h in range(2):
            nc.vector.quantize_mx(hid_w[h][:].bitcast(E5M2), hid_s[h][:], hid[h][:])
        for h in range(2):
            reads = slice(h * HALF, (h + 1) * HALF)
            for u in range(2):
                cols = slice(u * P, (u + 1) * P)
                nc.tensor.matmul_mx(y_ps[h][:, u, :], wb_w[:, cols].bitcast(E4M3), wb_plane[:, cols], hid_w[h][:].bitcast(E5M2), hid_s[h][:], start=False, stop=(u == 1))
            y_sb = sb("y_sb%d" % h, [P, 2, HALF], F32)
            nc.scalar.copy(y_sb[:], y_ps[h][:])
            nc.sync.dma_start(out[:, reads].rearrange("(u p) o -> p u o", p=P), y_sb[:])
